import numpy as np
import ml_dtypes


def mxq(x, axis, fmt="e4m3"):
    dtype, down = {"e4m3": (ml_dtypes.float8_e4m3fn, 7), "e5m2": (ml_dtypes.float8_e5m2, 14)}[fmt]
    v = np.moveaxis(np.asarray(x, np.float32).astype(ml_dtypes.bfloat16).astype(np.float64), axis, -1)
    blocks = v.reshape(v.shape[:-1] + (-1, 32))
    amax = np.abs(blocks).max(-1, keepdims=True)
    byte = np.maximum(np.where(amax > 0, np.frexp(amax)[1] - 1 + 127, 0) - down, 1)
    scale = np.exp2(byte - 127.0)
    codes = (blocks / scale).astype(np.float32).astype(dtype).astype(np.float64)
    return np.moveaxis((codes * scale).reshape(v.shape), -1, axis)


WIDE = False


def mx_kscale(k):
    if not WIDE:
        return np.ones(k)
    levels = np.array([10, -10, 5, -5, 0])
    if k % 512:
        return np.exp2(np.random.permutation(np.resize(levels, k // 32))).repeat(32)
    a = np.empty((k // 512, 16))
    for p in range(k // 512):
        a[p, :8] = np.random.permutation(np.resize(levels, 8))
        for g in range(8):
            far = levels[np.abs(levels - a[p, g]) >= 10]
            a[p, g + 8] = far[np.random.randint(len(far))]
    return np.exp2(a.ravel()).repeat(32)


def f64(x):
    return np.asarray(x).astype(np.float64)


def striped(idx):
    return np.tile(np.asarray(idx).reshape(-1, 16).T, (8, 1)).astype(np.uint16)


def unstriped(offs):
    return offs[:16].T.reshape(-1).astype(np.int64)


E2M1 = np.array([0.0, 0.5, 1.0, 1.5, 2.0, 3.0, 4.0, 6.0, -0.0, -0.5, -1.0, -1.5, -2.0, -3.0, -4.0, -6.0])


def pack_weight(w, fmt):
    k, n = w.shape
    w = f64(np.asarray(w, np.float32).astype(ml_dtypes.bfloat16)).reshape(k // 32, 32, n)
    amax = np.abs(w).max(1)
    if fmt == "e4m3":
        byte = np.frexp(amax)[1] - 1 + 127 - 7
    else:
        mant, ex = np.frexp(amax / 6.0)
        byte = np.where(mant > 0.5, ex, ex - 1) + 127
    byte = np.clip(np.where(amax > 0, byte, 1), 1, 254)
    scaled = (w * np.exp2(127.0 - byte)[:, None, :]).reshape(k, n).astype(np.float32)
    by_word = np.ascontiguousarray(scaled.reshape(k // 512, 128, 4, n).transpose(0, 1, 3, 2))
    if fmt == "e4m3":
        words = by_word.astype(ml_dtypes.float8_e4m3fn).view(np.uint8)
    else:
        c = by_word.astype(ml_dtypes.float4_e2m1fn).view(np.uint8) & 0xF
        words = (c[..., 0::2] | (c[..., 1::2] << 4)).reshape(k // 512, 128, 2 * n)
    return np.ascontiguousarray(words), np.ascontiguousarray(byte.astype(np.uint8).reshape(k // 512, 16, n))


def unpack_weight(words, scales, fmt):
    g, _, n = scales.shape
    words = np.ascontiguousarray(words).reshape(g, 128, n, -1)
    if fmt == "e4m3":
        vals = words.view(ml_dtypes.float8_e4m3fn).astype(np.float64)
    else:
        nib = np.empty((g, 128, n, 4), np.uint8)
        nib[..., 0::2] = words & 0xF
        nib[..., 1::2] = words >> 4
        vals = E2M1[nib]
    vals = vals * np.repeat(np.exp2(scales.astype(np.float64) - 127.0), 8, axis=1)[..., None]
    return vals.transpose(0, 1, 3, 2).reshape(g * 512, n)


def sigmoid(v):
    return 1.0 / (1.0 + np.exp(-v))


D, E, T, I, Q = 512, 512, 1024, 256, 512


def setup_inputs():
    n = np.random.standard_normal
    idx = np.random.permutation(T)[:I]
    idx2 = np.random.permutation(T)[:I]
    fd = mx_kscale(D)
    fq = mx_kscale(Q)
    keysp = pack_weight(n((D, T)) / fd[:, None], "e2m1")
    return {
        "query": (n((D, Q)) * 0.5 / np.sqrt(D) * fd[:, None]).astype(np.float32),
        "qs": (np.random.uniform(8.0, 32.0, (Q, 1)) * fq[:, None]).astype(np.float32),
        "grows": (n((Q, E)) / fq[:, None]).astype(np.float32),
        "vals": (n((E, T))).astype(np.float32),
        "keys_words": keysp[0],
        "keys_scales": keysp[1],
        "fr": (np.random.uniform(0.2, 0.8, (1, I))).astype(np.float32),
        "sg": (np.random.uniform(0.5, 2.0, (1, I))).astype(np.float32),
        "old": (n((E, T)) * 1.0).astype(np.float32),
        "fade": (np.random.uniform(0.5, 1.0, (1, T))).astype(np.float32),
        "offs": striped(idx),
        "offs2": striped(idx2),
    }


def reference(query, qs, grows, vals, keys_words, keys_scales, fr, sg, old, fade, offs, offs2):
    idx = unstriped(offs)
    idx2 = unstriped(offs2)
    keysu = unpack_weight(keys_words, keys_scales, "e2m1")
    queryq = mxq(f64(query), 0, "e4m3")
    keysidxg = keysu[:, idx]
    a = queryq.T @ keysidxg
    p = np.exp(a - np.max(a, axis=1, keepdims=True))
    w = p * f64(qs) / np.sum(p, axis=1, keepdims=True)
    growsq = mxq(f64(grows), 0, "e4m3")
    wq = mxq(w, 0, "e4m3")
    c0 = growsq.T @ wq
    x1 = f64(vals)[:, idx] * (1.0 - f64(fr)) + f64(vals)[:, idx2] * f64(fr)
    dx1 = c0 * sigmoid(x1) * (1.0 + x1 * (1.0 - sigmoid(x1)))
    gs = dx1 * f64(sg)
    gf = np.zeros((E, T))
    gf[:, idx] = gs
    y = f64(old) * f64(fade) + gf
    return y

@@ -1,0 +1,249 @@
+from contextlib import ExitStack
+
+import concourse.mybir as mybir
+from concourse.masks import make_identity
+
+D, E, T, I, Q = 512, 512, 1024, 256, 512
+FLOPS = 2 * Q * I * D + 2 * E * I * Q
+
+F32 = mybir.dt.float32
+BF16 = mybir.dt.bfloat16
+I32 = mybir.dt.int32
+U32 = mybir.dt.uint32
+U16 = mybir.dt.uint16
+U8 = mybir.dt.uint8
+FP8X4 = mybir.dt.float8_e4m3fn_x4
+FP4X4 = mybir.dt.float4_e2m1fn_x4
+ALU = mybir.AluOpType
+ACT = mybir.ActivationFunctionType
+AX = mybir.AxisListType
+
+P = 128
+PACK = 4
+TILES = E // P
+HALF = T // 2
+
+
+def tile_attend_bvbetween_s_kernel(tc, query, qs, grows, vals, keys_words, keys_scales, fr, sg, old, fade, offs, offs2, out):
+    nc = tc.nc
+    with ExitStack() as ctx:
+        keep = ctx.enter_context(tc.tile_pool(name="keep", bufs=1))
+        psum = ctx.enter_context(tc.psum_pool(name="psum", bufs=1))
+
+        def sb(shape, dtype, name):
+            return keep.tile(shape, dtype, name=name, align_bytes=64)
+
+        def bank(name):
+            return psum.tile([P, 512], F32, name=name, tag="ring", bufs=6)
+
+        def turn(dst, src, start=True, stop=True):
+            nc.tensor.matmul(dst, lhsT=src, rhs=ident[:], start=start, stop=stop, is_transpose=True)
+
+        list1 = sb([P, I // 16], U16, "list1")
+        list2 = sb([P, I // 16], U16, "list2")
+        key_words = sb([P, T], U16, "key_words")
+        key_bytes = sb([P, T], U8, "key_bytes")
+        fade_rows = sb([P, P], F32, "fade_rows")
+        fr_rows = sb([P, I], F32, "fr_rows")
+        sg_rows = sb([P, I], F32, "sg_rows")
+        q_raw = sb([P, PACK, Q], F32, "q_raw")
+        g_raw = sb([P, PACK, E], F32, "g_raw")
+        qs_cols = sb([P, PACK], F32, "qs_cols")
+        val_t = [sb([P, T], F32, "val%d" % k) for k in range(TILES)]
+        old_t = [[sb([P, 2, HALF], F32, "old%d_%d" % (h, u)) for u in range(2)] for h in range(2)]
+        put = [sb([P, T], F32, "put%d" % k) for k in range(TILES)]
+        ident = sb([P, P], F32, "ident")
+        warm = sb([P, 8], F32, "warm")
+        warm_out = sb([P, 8], F32, "warm_out")
+
+        nc.vector.memset(key_bytes[:].bitcast(I32), 0)
+        nc.vector.memset(warm[:], 0.0)
+        nc.vector.memset(fade_rows[:], 0.0)
+        nc.scalar.activation(warm_out[:], warm[:], ACT.Exp)
+        make_identity(nc, ident[:])
+
+        nc.sync.dma_start(list1[:], offs)
+        nc.sync.dma_start(out=fr_rows[:], in_=fr[0].partition_broadcast(P))
+        nc.sync.dma_start(out=val_t[0][:], in_=vals[0:P, :])
+        nc.sync.dma_start(list2[:], offs2)
+        nc.sync.dma_start(out=key_words[:].bitcast(I32), in_=keys_words[0].bitcast(I32))
+        for g in range(4):
+            nc.sync.dma_start(out=key_bytes[32 * g : 32 * g + 4, :].bitcast(I32), in_=keys_scales[0, 4 * g : 4 * g + 4, :].bitcast(I32))
+        nc.sync.dma_start(out=q_raw[:], in_=query.rearrange("(p j) q -> p j q", j=PACK))
+        nc.sync.dma_start(out=val_t[1][:], in_=vals[P : 2 * P, :])
+        nc.sync.dma_start(out=qs_cols[:], in_=qs.rearrange("(p r) o -> p (r o)", r=PACK))
+        nc.sync.dma_start(out=g_raw[:], in_=grows.rearrange("(p j) e -> p j e", j=PACK))
+        nc.sync.dma_start(out=sg_rows[:], in_=sg[0].partition_broadcast(P))
+        nc.sync.dma_start(out=val_t[2][:], in_=vals[2 * P : 3 * P, :])
+        nc.sync.dma_start(out=fade_rows[0:8, :], in_=fade.rearrange("o (j p) -> (o j) p", p=P))
+        nc.sync.dma_start(out=val_t[3][:], in_=vals[3 * P : 4 * P, :])
+        for h in range(2):
+            for u in range(2):
+                nc.sync.dma_start(
+                    out=old_t[h][u][:],
+                    in_=old[2 * P * u : 2 * P * (u + 1), HALF * h : HALF * (h + 1)].rearrange("(k p) t -> p k t", p=P),
+                )
+
+        for k in range(TILES):
+            nc.vector.memset(put[k][:], 0.0)
+
+        fa = sb([P, I], F32, "fa")
+        fb = sb([P, I], F32, "fb")
+        nc.vector.tensor_scalar(fa[:], fr_rows[:], 0.5, -0.5, ALU.mult, ALU.add)
+        nc.vector.tensor_scalar(fb[:], fr_rows[:], -0.5, None, ALU.mult)
+
+        slope = [None] * TILES
+
+        def gather(k):
+            ga = sb([P, I], F32, "ga%d" % k)
+            gb = sb([P, I], F32, "gb%d" % k)
+            nc.vector.tensor_tensor(ga[:], val_t[k][:].indirect(list1[:]), fa[:], ALU.mult)
+            nc.vector.tensor_tensor(gb[:], val_t[k][:].indirect(list2[:]), fb[:], ALU.mult)
+            xb = bank("xb%d" % k)
+            for h in range(2):
+                cols = slice(P * h, P * (h + 1))
+                turn(xb[:, cols], ga[:, cols], True, False)
+                turn(xb[:, cols], gb[:, cols], False, True)
+            th = sb([P, I], F32, "th%d" % k)
+            sq = sb([P, I], F32, "sq%d" % k)
+            nc.scalar.activation(th[:], xb[:, 0:I], ACT.Tanh, scale=-1.0)
+            nc.scalar.activation(sq[:], th[:], ACT.Square)
+            return xb, th, sq
+
+        def chain(k, xb, th, sq):
+            tt = sb([P, I], F32, "tt%d" % k)
+            nc.vector.scalar_tensor_tensor(tt[:], sq[:], 1.0, xb[:, 0:I], ALU.subtract, ALU.mult)
+            fbk = bank("fbk%d" % k)
+            for h in range(2):
+                cols = slice(P * h, P * (h + 1))
+                turn(fbk[:, cols], th[:, cols], True, False)
+                turn(fbk[:, cols], tt[:, cols], False, True)
+            return fbk
+
+        def finish(k, fbk):
+            s = sb([P, I], F32, "slope%d" % k)
+            nc.vector.scalar_tensor_tensor(s[:], fbk[:, 0:I], 1.0, sg_rows[:], ALU.add, ALU.mult)
+            slope[k] = s
+
+        st0 = gather(0)
+
+        kw = sb([P, I], U16, "kw")
+        kb = sb([P, I], U8, "kb")
+        nc.vector.tensor_copy(kw[:], key_words[:].indirect(list1[:]))
+        nc.vector.tensor_copy(kb[:], key_bytes[:].indirect(list1[:]))
+
+        q_bf = sb([P, PACK, P, PACK], BF16, "q_bf")
+        q_src = q_raw[:].rearrange("p j (s r) -> p s j r", r=PACK)
+        q_dst = q_bf[:].rearrange("p r s j -> p s j r")
+        cut = 80
+        nc.vector.tensor_copy(q_dst[:, 0:cut], q_src[:, 0:cut])
+        nc.scalar.copy(q_dst[:, cut:P], q_src[:, cut:P])
+        q_codes = sb([P, Q], U32, "q_codes")
+        q_bytes = sb([P, Q], U8, "q_bytes")
+        nc.vector.quantize_mx(out=q_codes[:].bitcast(FP8X4), scales=q_bytes[:], in_=q_bf[:].rearrange("p r s j -> p (r s j)"))
+
+        fb0 = chain(0, *st0)
+        st1 = gather(1)
+
+        scores = [psum.tile([P, 2, I], F32, name="scores%d" % b, tag="prod", bufs=2) for b in range(2)]
+        for r in range(PACK):
+            cols = slice(P * r, P * (r + 1))
+            nc.tensor.matmul_mx(
+                out=scores[r // 2][:, r % 2, :], lhsT=q_codes[:, cols].bitcast(FP8X4), lhsT_scale=q_bytes[:, cols],
+                rhs=kw[:].bitcast(FP4X4), rhs_scale=kb[:], start=True, stop=True,
+            )
+        neg_max = [sb([P, 2], F32, "neg_max%d" % b) for b in range(2)]
+        sums = sb([P, PACK], F32, "sums")
+        probs = sb([P, PACK, I], F32, "probs")
+        for b in range(2):
+            nc.vector.tensor_reduce(neg_max[b][:], scores[b][:], AX.X, ALU.max, negate=True)
+            for u in range(2):
+                r = 2 * b + u
+                nc.scalar.activation(
+                    probs[:, r, :], scores[b][:, u, :], ACT.Exp, bias=neg_max[b][:, u : u + 1], accum_out=sums[:, r : r + 1]
+                )
+        finish(0, fb0)
+        fb1 = chain(1, *st1)
+
+        g_bf = sb([P, E, PACK], BF16, "g_bf")
+        g_codes = sb([P, E], U32, "g_codes")
+        g_bytes = sb([P, E], U8, "g_bytes")
+        g_src = g_raw[:].rearrange("p j (c i) -> p c j i", i=PACK)
+        g_dst = g_bf[:].rearrange("p (c i) j -> p c j i", i=PACK)
+        nc.scalar.copy(g_dst, g_src)
+
+        inv = sb([P, PACK], F32, "inv")
+        row_f = sb([P, PACK], F32, "row_f")
+        nc.vector.reciprocal(inv[:], sums[:])
+        nc.vector.tensor_tensor(row_f[:], inv[:], qs_cols[:], ALU.mult)
+        w_bf = sb([P, I, PACK], BF16, "w_bf")
+        nc.vector.tensor_tensor(
+            w_bf[:].rearrange("p (c i) r -> p c r i", i=PACK),
+            probs[:].rearrange("p r (c i) -> p c r i", i=PACK),
+            row_f[:].unsqueeze(1).unsqueeze(3).broadcast_to([P, I // PACK, PACK, PACK]),
+            ALU.mult,
+        )
+        w_codes = sb([P, I], U32, "w_codes")
+        w_bytes = sb([P, I], U8, "w_bytes")
+        finish(1, fb1)
+        nc.vector.quantize_mx(out=w_codes[:].bitcast(FP8X4), scales=w_bytes[:], in_=w_bf[:].rearrange("p i r -> p (i r)"))
+        nc.vector.quantize_mx(out=g_codes[:].bitcast(FP8X4), scales=g_bytes[:], in_=g_bf[:].rearrange("p e j -> p (e j)"))
+
+        grads = [psum.tile([P, 2, I], F32, name="grads%d" % b, tag="prod", bufs=2) for b in range(2)]
+        c0 = []
+        for k in range(TILES):
+            cols = slice(P * k, P * (k + 1))
+            nc.tensor.matmul_mx(
+                out=grads[k // 2][:, k % 2, :], lhsT=g_codes[:, cols].bitcast(FP8X4), lhsT_scale=g_bytes[:, cols],
+                rhs=w_codes[:].bitcast(FP8X4), rhs_scale=w_bytes[:], start=True, stop=True,
+            )
+        for b in range(2):
+            for u in range(2):
+                c = sb([P, I], F32, "c0_%d" % (2 * b + u))
+                nc.scalar.activation(c[:], grads[b][:, u, :], ACT.Copy, scale=0.5)
+                c0.append(c)
+
+        st2 = gather(2)
+        st3 = gather(3)
+
+        def scatter(k):
+            nc.vector.tensor_tensor(put[k][:].indirect(list1[:]), c0[k][:], slope[k][:], ALU.mult)
+
+        fb2 = chain(2, *st2)
+        scatter(0)
+        fb3 = chain(3, *st3)
+        finish(2, fb2)
+        scatter(1)
+        finish(3, fb3)
+
+        fc_bank = bank("fc_bank")
+        turn(fc_bank[:, 0:P], fade_rows[:])
+        fade_cols = sb([P, 8], F32, "fade_cols")
+        nc.scalar.copy(fade_cols[:], fc_bank[:, 0:8])
+
+        faded = [sb([P, E], F32, "faded%d" % j) for j in range(8)]
+        for j in range(8):
+            h, jj = j // 4, j % 4
+            ob = bank("ob%d" % j)
+            for k in range(TILES):
+                turn(ob[:, P * k : P * (k + 1)], old_t[h][k // 2][:, k % 2, P * jj : P * (jj + 1)])
+            nc.scalar.activation(faded[j][:], ob[:], ACT.Copy, scale=fade_cols[:, j : j + 1])
+
+        def add_store(k, h):
+            back = bank("back%d_%d" % (k, h))
+            for jj in range(4):
+                turn(back[:, P * jj : P * (jj + 1)], faded[4 * h + jj][:, P * k : P * (k + 1)])
+            res = sb([P, HALF], F32, "res%d_%d" % (k, h))
+            nc.vector.tensor_tensor(res[:], back[:], put[k][:, HALF * h : HALF * (h + 1)], ALU.add)
+            nc.sync.dma_start(out=out[P * k : P * (k + 1), HALF * h : HALF * (h + 1)], in_=res[:])
+
+        add_store(0, 0)
+        add_store(1, 0)
+        scatter(2)
+        add_store(0, 1)
+        add_store(1, 1)
+        add_store(2, 0)
+        add_store(2, 1)
+        scatter(3)
+        add_store(3, 0)
+        add_store(3, 1)

@@ -20,37 +20,63 @@ AX = mybir.AxisListType
 
 P = 128
 PACK = 4
+BANK = 512
 TILES = E // P
 HALF = T // 2
+BLOCKS = T // P
+POOL_TILES = 2
+TURNED = TILES - POOL_TILES
+QUERY_SPLIT = 64
 
 
-def tile_attend_bvbetween_s_kernel(tc, query, qs, grows, vals, keys_words, keys_scales, fr, sg, old, fade, offs, offs2, out):
+def tile_attend_bvbetween_s_kernel(
+    tc, query, qs, grows, vals, keys_words, keys_scales, fr, sg, old, fade, offs, offs2, out
+):
     nc = tc.nc
     with ExitStack() as ctx:
         keep = ctx.enter_context(tc.tile_pool(name="keep", bufs=1))
         psum = ctx.enter_context(tc.psum_pool(name="psum", bufs=1))
 
-        def sb(shape, dtype, name):
-            return keep.tile(shape, dtype, name=name, align_bytes=64)
+        def sb(shape, dtype, name, on=None):
+            return keep.tile(shape, dtype, name=name, tag=on or name, align_bytes=64)
 
-        def bank(name):
-            return psum.tile([P, 512], F32, name=name, tag="ring", bufs=6)
+        def bank(name, ring):
+            return psum.tile([P, BANK], F32, name=name, tag=ring, bufs=4 if ring == "mix" else 2)
+
+        def span(n, width):
+            return slice(n * width, (n + 1) * width)
 
         def turn(dst, src, start=True, stop=True):
             nc.tensor.matmul(dst, lhsT=src, rhs=ident[:], start=start, stop=stop, is_transpose=True)
+
+        def turn_sum(dst, first, second):
+            for b in range(2):
+                turn(dst[:, span(b, P)], first[:, span(b, P)], True, False)
+                turn(dst[:, span(b, P)], second[:, span(b, P)], False, True)
+
+        def spread(dst, cols):
+            for c in range(cols.shape[1]):
+                turn(dst[:, span(c, P)], cols[:, c : c + 1].to_broadcast([P, P]))
+
+        def quantise(name, src, codes=None, scales=None):
+            if codes is None:
+                codes = sb([P, src.shape[1] // PACK], U32, name + "_codes")[:]
+                scales = sb([P, src.shape[1] // PACK], U8, name + "_scales")[:]
+            nc.vector.quantize_mx(out=codes.bitcast(FP8X4), scales=scales, in_=src)
+            return codes, scales
 
         list1 = sb([P, I // 16], U16, "list1")
         list2 = sb([P, I // 16], U16, "list2")
         key_words = sb([P, T], U16, "key_words")
         key_bytes = sb([P, T], U8, "key_bytes")
-        fade_rows = sb([P, P], F32, "fade_rows")
-        fr_rows = sb([P, I], F32, "fr_rows")
-        sg_rows = sb([P, I], F32, "sg_rows")
+        small_rows = sb([P, P], F32, "small_rows")
+        fr_pairs = sb([P, 2], F32, "fr_pairs")
         q_raw = sb([P, PACK, Q], F32, "q_raw")
         g_raw = sb([P, PACK, E], F32, "g_raw")
         qs_cols = sb([P, PACK], F32, "qs_cols")
-        val_t = [sb([P, T], F32, "val%d" % k) for k in range(TILES)]
-        old_t = [[sb([P, 2, HALF], F32, "old%d_%d" % (h, u)) for u in range(2)] for h in range(2)]
+        val = [sb([P, T], F32, "val%d" % k) for k in range(TILES)]
+        old_pool = [sb([P, T], F32, "old_pool%d" % k) for k in range(POOL_TILES)]
+        old_turn = [sb([P, TURNED, HALF], F32, "old_turn%d" % h) for h in range(2)]
         put = [sb([P, T], F32, "put%d" % k) for k in range(TILES)]
         ident = sb([P, P], F32, "ident")
         warm = sb([P, 8], F32, "warm")
@@ -58,192 +84,217 @@ def tile_attend_bvbetween_s_kernel(tc, query, qs, grows, vals, keys_words, keys_
 
         nc.vector.memset(key_bytes[:].bitcast(I32), 0)
         nc.vector.memset(warm[:], 0.0)
-        nc.vector.memset(fade_rows[:], 0.0)
+        nc.vector.memset(small_rows[:], 0.0)
         nc.scalar.activation(warm_out[:], warm[:], ACT.Exp)
         make_identity(nc, ident[:])
 
+        def load_val(k):
+            nc.sync.dma_start(out=val[k][:], in_=vals[span(k, P), :])
+
+        nc.sync.dma_start(out=fr_pairs[:], in_=fr.rearrange("o (p h) -> p (o h)", h=2))
         nc.sync.dma_start(list1[:], offs)
-        nc.sync.dma_start(out=fr_rows[:], in_=fr[0].partition_broadcast(P))
-        nc.sync.dma_start(out=val_t[0][:], in_=vals[0:P, :])
         nc.sync.dma_start(list2[:], offs2)
+        load_val(0)
         nc.sync.dma_start(out=key_words[:].bitcast(I32), in_=keys_words[0].bitcast(I32))
+        load_val(1)
         for g in range(4):
-            nc.sync.dma_start(out=key_bytes[32 * g : 32 * g + 4, :].bitcast(I32), in_=keys_scales[0, 4 * g : 4 * g + 4, :].bitcast(I32))
+            nc.sync.dma_start(
+                out=key_bytes[32 * g : 32 * g + 4, :].bitcast(I32), in_=keys_scales[0, span(g, 4), :].bitcast(I32)
+            )
         nc.sync.dma_start(out=q_raw[:], in_=query.rearrange("(p j) q -> p j q", j=PACK))
-        nc.sync.dma_start(out=val_t[1][:], in_=vals[P : 2 * P, :])
-        nc.sync.dma_start(out=qs_cols[:], in_=qs.rearrange("(p r) o -> p (r o)", r=PACK))
+        load_val(2)
         nc.sync.dma_start(out=g_raw[:], in_=grows.rearrange("(p j) e -> p j e", j=PACK))
-        nc.sync.dma_start(out=sg_rows[:], in_=sg[0].partition_broadcast(P))
-        nc.sync.dma_start(out=val_t[2][:], in_=vals[2 * P : 3 * P, :])
-        nc.sync.dma_start(out=fade_rows[0:8, :], in_=fade.rearrange("o (j p) -> (o j) p", p=P))
-        nc.sync.dma_start(out=val_t[3][:], in_=vals[3 * P : 4 * P, :])
+        nc.sync.dma_start(out=small_rows[BLOCKS : BLOCKS + 2, :], in_=sg.rearrange("o (j p) -> (o j) p", p=P))
+        nc.sync.dma_start(out=small_rows[0:BLOCKS, :], in_=fade.rearrange("o (j p) -> (o j) p", p=P))
+        nc.sync.dma_start(out=qs_cols[:], in_=qs.rearrange("(p r) o -> p (r o)", r=PACK))
+        load_val(3)
+        for k in range(POOL_TILES):
+            nc.sync.dma_start(out=old_pool[k][:], in_=old[span(k, P), :])
         for h in range(2):
-            for u in range(2):
-                nc.sync.dma_start(
-                    out=old_t[h][u][:],
-                    in_=old[2 * P * u : 2 * P * (u + 1), HALF * h : HALF * (h + 1)].rearrange("(k p) t -> p k t", p=P),
-                )
+            nc.sync.dma_start(
+                out=old_turn[h][:], in_=old[POOL_TILES * P : E, span(h, HALF)].rearrange("(k p) t -> p k t", p=P)
+            )
 
-        for k in range(TILES):
-            nc.vector.memset(put[k][:], 0.0)
+        for k in range(2):
+            nc.vector.memset(put[k][:].bitcast(I32), 0)
+            nc.gpsimd.memset(put[2 + k][:], 0.0)
 
-        fa = sb([P, I], F32, "fa")
-        fb = sb([P, I], F32, "fb")
-        nc.vector.tensor_scalar(fa[:], fr_rows[:], 0.5, -0.5, ALU.mult, ALU.add)
-        nc.vector.tensor_scalar(fb[:], fr_rows[:], -0.5, None, ALU.mult)
+        share1 = sb([P, I], F32, "share1")
+        share2 = sb([P, I], F32, "share2")
+        fr_bank = bank("fr_bank", "misc")
+        spread(fr_bank, fr_pairs[:])
+        fr_rows = fr_bank[:, 0:I].rearrange("p (h n) -> p n h", h=2)
+        nc.scalar.activation(share1[:].rearrange("p (n h) -> p n h", h=2), fr_rows, ACT.Copy, scale=0.5, bias=-0.5)
+        nc.scalar.activation(share2[:].rearrange("p (n h) -> p n h", h=2), fr_rows, ACT.Copy, scale=-0.5)
 
+        mix_bank = [None] * TILES
+        curve = [None] * TILES
         slope = [None] * TILES
 
-        def gather(k):
-            ga = sb([P, I], F32, "ga%d" % k)
-            gb = sb([P, I], F32, "gb%d" % k)
-            nc.vector.tensor_tensor(ga[:], val_t[k][:].indirect(list1[:]), fa[:], ALU.mult)
-            nc.vector.tensor_tensor(gb[:], val_t[k][:].indirect(list2[:]), fb[:], ALU.mult)
-            xb = bank("xb%d" % k)
-            for h in range(2):
-                cols = slice(P * h, P * (h + 1))
-                turn(xb[:, cols], ga[:, cols], True, False)
-                turn(xb[:, cols], gb[:, cols], False, True)
-            th = sb([P, I], F32, "th%d" % k)
-            sq = sb([P, I], F32, "sq%d" % k)
-            nc.scalar.activation(th[:], xb[:, 0:I], ACT.Tanh, scale=-1.0)
-            nc.scalar.activation(sq[:], th[:], ACT.Square)
-            return xb, th, sq
+        def gather_vals(k):
+            parts = sb([P, 2, I], F32, "parts%d" % k)
+            nc.vector.tensor_tensor(parts[:, 0, :], val[k][:].indirect(list1[:]), share1[:], ALU.mult)
+            nc.vector.tensor_tensor(parts[:, 1, :], val[k][:].indirect(list2[:]), share2[:], ALU.mult)
+            mix_bank[k] = bank("mix%d" % k, "mix")
+            turn_sum(mix_bank[k][:, 0:I], parts[:, 0, :], parts[:, 1, :])
 
-        def chain(k, xb, th, sq):
-            tt = sb([P, I], F32, "tt%d" % k)
-            nc.vector.scalar_tensor_tensor(tt[:], sq[:], 1.0, xb[:, 0:I], ALU.subtract, ALU.mult)
-            fbk = bank("fbk%d" % k)
-            for h in range(2):
-                cols = slice(P * h, P * (h + 1))
-                turn(fbk[:, cols], th[:, cols], True, False)
-                turn(fbk[:, cols], tt[:, cols], False, True)
-            return fbk
+        def tanh_and_square(k, room):
+            curve[k] = room
+            nc.scalar.activation(room[:, 0, :], mix_bank[k][:, 0:I], ACT.Tanh, scale=-1.0)
+            nc.scalar.activation(room[:, 1, :], room[:, 0, :], ACT.Square)
 
-        def finish(k, fbk):
-            s = sb([P, I], F32, "slope%d" % k)
-            nc.vector.scalar_tensor_tensor(s[:], fbk[:, 0:I], 1.0, sg_rows[:], ALU.add, ALU.mult)
-            slope[k] = s
+        def bend(k):
+            room = curve[k]
+            nc.vector.scalar_tensor_tensor(room[:, 2, :], room[:, 1, :], 1.0, mix_bank[k][:, 0:I], ALU.subtract, ALU.mult)
+            turn_sum(mix_bank[k][:, I:BANK], room[:, 0, :], room[:, 2, :])
 
-        st0 = gather(0)
+        def finish_slope(k):
+            slope[k] = sb([P, I], F32, "slope%d" % k)
+            nc.vector.scalar_tensor_tensor(slope[k][:], mix_bank[k][:, I:BANK], 1.0, half_gain[:], ALU.add, ALU.mult)
 
-        kw = sb([P, I], U16, "kw")
-        kb = sb([P, I], U8, "kb")
-        nc.vector.tensor_copy(kw[:], key_words[:].indirect(list1[:]))
-        nc.vector.tensor_copy(kb[:], key_bytes[:].indirect(list1[:]))
+        gather_vals(0)
+        gather_vals(1)
+        keys_w = sb([P, I], U16, "keys_w")
+        keys_b = sb([P, I], U8, "keys_b")
+        nc.vector.tensor_copy(keys_w[:], key_words[:].indirect(list1[:]))
+        nc.vector.tensor_copy(keys_b[:], key_bytes[:].indirect(list1[:]))
 
         q_bf = sb([P, PACK, P, PACK], BF16, "q_bf")
         q_src = q_raw[:].rearrange("p j (s r) -> p s j r", r=PACK)
         q_dst = q_bf[:].rearrange("p r s j -> p s j r")
-        cut = 80
-        nc.vector.tensor_copy(q_dst[:, 0:cut], q_src[:, 0:cut])
-        nc.scalar.copy(q_dst[:, cut:P], q_src[:, cut:P])
-        q_codes = sb([P, Q], U32, "q_codes")
-        q_bytes = sb([P, Q], U8, "q_bytes")
-        nc.vector.quantize_mx(out=q_codes[:].bitcast(FP8X4), scales=q_bytes[:], in_=q_bf[:].rearrange("p r s j -> p (r s j)"))
+        nc.vector.tensor_copy(q_dst[:, 0:QUERY_SPLIT], q_src[:, 0:QUERY_SPLIT])
+        nc.scalar.copy(q_dst[:, QUERY_SPLIT:P], q_src[:, QUERY_SPLIT:P])
+        q_codes, q_scales = quantise("q", q_bf[:].rearrange("p r s j -> p (r s j)"))
 
-        fb0 = chain(0, *st0)
-        st1 = gather(1)
-
-        scores = [psum.tile([P, 2, I], F32, name="scores%d" % b, tag="prod", bufs=2) for b in range(2)]
+        scores = [bank("scores%d" % b, "prod")[:].rearrange("p (u i) -> p u i", u=2) for b in range(2)]
         for r in range(PACK):
-            cols = slice(P * r, P * (r + 1))
             nc.tensor.matmul_mx(
-                out=scores[r // 2][:, r % 2, :], lhsT=q_codes[:, cols].bitcast(FP8X4), lhsT_scale=q_bytes[:, cols],
-                rhs=kw[:].bitcast(FP4X4), rhs_scale=kb[:], start=True, stop=True,
+                out=scores[r // 2][:, r % 2, :],
+                lhsT=q_codes[:, span(r, P)].bitcast(FP8X4),
+                lhsT_scale=q_scales[:, span(r, P)],
+                rhs=keys_w[:].bitcast(FP4X4),
+                rhs_scale=keys_b[:],
+                start=True,
+                stop=True,
             )
-        neg_max = [sb([P, 2], F32, "neg_max%d" % b) for b in range(2)]
         sums = sb([P, PACK], F32, "sums")
         probs = sb([P, PACK, I], F32, "probs")
         for b in range(2):
-            nc.vector.tensor_reduce(neg_max[b][:], scores[b][:], AX.X, ALU.max, negate=True)
+            neg_max = sb([P, 2], F32, "neg_max%d" % b)
+            nc.vector.tensor_reduce(neg_max[:], scores[b], AX.X, ALU.max, negate=True)
             for u in range(2):
                 r = 2 * b + u
                 nc.scalar.activation(
-                    probs[:, r, :], scores[b][:, u, :], ACT.Exp, bias=neg_max[b][:, u : u + 1], accum_out=sums[:, r : r + 1]
+                    probs[:, r, :], scores[b][:, u, :], ACT.Exp, bias=neg_max[:, u : u + 1], accum_out=sums[:, r : r + 1]
                 )
-        finish(0, fb0)
-        fb1 = chain(1, *st1)
-
-        g_bf = sb([P, E, PACK], BF16, "g_bf")
-        g_codes = sb([P, E], U32, "g_codes")
-        g_bytes = sb([P, E], U8, "g_bytes")
-        g_src = g_raw[:].rearrange("p j (c i) -> p c j i", i=PACK)
-        g_dst = g_bf[:].rearrange("p (c i) j -> p c j i", i=PACK)
-        nc.scalar.copy(g_dst, g_src)
 
         inv = sb([P, PACK], F32, "inv")
-        row_f = sb([P, PACK], F32, "row_f")
         nc.vector.reciprocal(inv[:], sums[:])
-        nc.vector.tensor_tensor(row_f[:], inv[:], qs_cols[:], ALU.mult)
-        w_bf = sb([P, I, PACK], BF16, "w_bf")
-        nc.vector.tensor_tensor(
-            w_bf[:].rearrange("p (c i) r -> p c r i", i=PACK),
-            probs[:].rearrange("p r (c i) -> p c r i", i=PACK),
-            row_f[:].unsqueeze(1).unsqueeze(3).broadcast_to([P, I // PACK, PACK, PACK]),
-            ALU.mult,
-        )
-        w_codes = sb([P, I], U32, "w_codes")
-        w_bytes = sb([P, I], U8, "w_bytes")
-        finish(1, fb1)
-        nc.vector.quantize_mx(out=w_codes[:].bitcast(FP8X4), scales=w_bytes[:], in_=w_bf[:].rearrange("p i r -> p (i r)"))
-        nc.vector.quantize_mx(out=g_codes[:].bitcast(FP8X4), scales=g_bytes[:], in_=g_bf[:].rearrange("p e j -> p (e j)"))
-
-        grads = [psum.tile([P, 2, I], F32, name="grads%d" % b, tag="prod", bufs=2) for b in range(2)]
-        c0 = []
-        for k in range(TILES):
-            cols = slice(P * k, P * (k + 1))
-            nc.tensor.matmul_mx(
-                out=grads[k // 2][:, k % 2, :], lhsT=g_codes[:, cols].bitcast(FP8X4), lhsT_scale=g_bytes[:, cols],
-                rhs=w_codes[:].bitcast(FP8X4), rhs_scale=w_bytes[:], start=True, stop=True,
+        w_rows = sb([P, PACK, I], BF16, "w_rows")
+        for r in range(PACK):
+            nc.vector.tensor_scalar(
+                w_rows[:, r, :], probs[:, r, :], inv[:, r : r + 1], qs_cols[:, r : r + 1], ALU.mult, ALU.mult
             )
-        for b in range(2):
-            for u in range(2):
-                c = sb([P, I], F32, "c0_%d" % (2 * b + u))
-                nc.scalar.activation(c[:], grads[b][:, u, :], ACT.Copy, scale=0.5)
-                c0.append(c)
+        w_bf = sb([P, I, PACK], BF16, "w_bf")
+        nc.vector.tensor_copy(
+            w_bf[:].rearrange("p (c i) r -> p c r i", i=PACK), w_rows[:].rearrange("p r (c i) -> p c r i", i=PACK)
+        )
+        w_codes, w_scales = quantise("w", w_bf[:].rearrange("p i r -> p (i r)"))
 
-        st2 = gather(2)
-        st3 = gather(3)
+        small_bank = bank("small_bank", "misc")
+        turn(small_bank[:, 0:P], small_rows[:])
+        gain_cols = sb([P, 2], F32, "gain_cols")
+        fade_cols = sb([P, BLOCKS], F32, "fade_cols")
+        nc.scalar.copy(gain_cols[:], small_bank[:, BLOCKS : BLOCKS + 2])
+        nc.scalar.copy(fade_cols[:], small_bank[:, 0:BLOCKS])
+        gain_bank = bank("gain_bank", "misc")
+        spread(gain_bank, gain_cols[:])
+        half_gain = sb([P, I], F32, "half_gain")
+        nc.scalar.activation(half_gain[:], gain_bank[:, 0:I], ACT.Copy, scale=0.5)
+
+        early = sb([P, 2, 3, I], F32, "early", "q_raw")
+        for k in (0, 1):
+            tanh_and_square(k, early[:, k])
+        gather_vals(2)
+        gather_vals(3)
+        for k in (0, 1):
+            bend(k)
+        for k in (0, 1):
+            finish_slope(k)
+
+        g_codes = sb([P, E], U32, "g_codes")
+        g_scales = sb([P, E], U8, "g_scales")
+        g_src = g_raw[:].rearrange("p j (n c i) -> p n c j i", n=TILES, i=PACK)
+        for u in range(2):
+            g_bf = sb([P, 2, P, PACK], BF16, "g_bf%d" % u)
+            for v in range(2):
+                nc.scalar.copy(g_bf[:, v].rearrange("p (c i) j -> p c j i", i=PACK), g_src[:, 2 * u + v])
+            cols = span(u, 2 * P)
+            quantise("g", g_bf[:].rearrange("p v e j -> p (v e j)"), g_codes[:, cols], g_scales[:, cols])
+
+        grads = [bank("grads%d" % u, "prod") for u in range(2)]
+        for k in range(TILES):
+            nc.tensor.matmul_mx(
+                out=grads[k // 2][:, span(k % 2, I)],
+                lhsT=g_codes[:, span(k, P)].bitcast(FP8X4),
+                lhsT_scale=g_scales[:, span(k, P)],
+                rhs=w_codes.bitcast(FP8X4),
+                rhs_scale=w_scales,
+                start=True,
+                stop=True,
+            )
+
+        late = sb([P, 2, 3, I], F32, "late")
+        for k in (2, 3):
+            tanh_and_square(k, late[:, k - 2])
+        for k in (2, 3):
+            bend(k)
+
+        fade_rows = sb([P, T], F32, "fade_rows")
+        for h in range(2):
+            rows = bank("fade_bank%d" % h, "misc")
+            spread(rows, fade_cols[:, span(h, 4)])
+            nc.scalar.copy(fade_rows[:, span(h, HALF)], rows[:])
+        for k in (2, 3):
+            finish_slope(k)
+
+        width = TURNED * P
+        faded = [sb([P, width], F32, "faded%d" % j) for j in range(BLOCKS)]
+        for pair in range(BLOCKS // 2):
+            turned = bank("turned%d" % pair, "misc")
+            for j in (2 * pair, 2 * pair + 1):
+                for v in range(TURNED):
+                    turn(turned[:, span(j % 2 * TURNED + v, P)], old_turn[j // 4][:, v, span(j % 4, P)])
+            for j in (2 * pair, 2 * pair + 1):
+                nc.scalar.activation(faded[j][:], turned[:, span(j % 2, width)], ACT.Copy, scale=fade_cols[:, j : j + 1])
 
         def scatter(k):
-            nc.vector.tensor_tensor(put[k][:].indirect(list1[:]), c0[k][:], slope[k][:], ALU.mult)
+            gs = sb([P, I], F32, "gs%d" % k)
+            nc.vector.tensor_tensor(gs[:], grads[k // 2][:, span(k % 2, I)], slope[k][:], ALU.mult)
+            nc.vector.tensor_copy(put[k][:].indirect(list1[:]), gs[:])
 
-        fb2 = chain(2, *st2)
-        scatter(0)
-        fb3 = chain(3, *st3)
-        finish(2, fb2)
-        scatter(1)
-        finish(3, fb3)
+        def sum_on_pool(k):
+            kept = sb([P, T], F32, "kept%d" % k, "w_bf" if k == 0 else None)
+            nc.gpsimd.tensor_tensor(kept[:], old_pool[k][:], fade_rows[:], ALU.mult)
+            for h in range(2):
+                res = sb([P, HALF], F32, "res%d_%d" % (k, h))
+                nc.gpsimd.tensor_tensor(res[:], kept[:, span(h, HALF)], put[k][:, span(h, HALF)], ALU.add)
+                nc.scalar.dma_start(out=out[span(k, P), span(h, HALF)], in_=res[:])
 
-        fc_bank = bank("fc_bank")
-        turn(fc_bank[:, 0:P], fade_rows[:])
-        fade_cols = sb([P, 8], F32, "fade_cols")
-        nc.scalar.copy(fade_cols[:], fc_bank[:, 0:8])
-
-        faded = [sb([P, E], F32, "faded%d" % j) for j in range(8)]
-        for j in range(8):
-            h, jj = j // 4, j % 4
-            ob = bank("ob%d" % j)
-            for k in range(TILES):
-                turn(ob[:, P * k : P * (k + 1)], old_t[h][k // 2][:, k % 2, P * jj : P * (jj + 1)])
-            nc.scalar.activation(faded[j][:], ob[:], ACT.Copy, scale=fade_cols[:, j : j + 1])
-
-        def add_store(k, h):
-            back = bank("back%d_%d" % (k, h))
-            for jj in range(4):
-                turn(back[:, P * jj : P * (jj + 1)], faded[4 * h + jj][:, P * k : P * (k + 1)])
+        def sum_on_vector(k, h):
+            back = bank("back%d_%d" % (k, h), "mix")
+            for j in range(4):
+                turn(back[:, span(j, P)], faded[4 * h + j][:, span(k - POOL_TILES, P)])
             res = sb([P, HALF], F32, "res%d_%d" % (k, h))
-            nc.vector.tensor_tensor(res[:], back[:], put[k][:, HALF * h : HALF * (h + 1)], ALU.add)
-            nc.sync.dma_start(out=out[P * k : P * (k + 1), HALF * h : HALF * (h + 1)], in_=res[:])
+            nc.vector.tensor_tensor(res[:], back[:], put[k][:, span(h, HALF)], ALU.add)
+            nc.sync.dma_start(out=out[span(k, P), span(h, HALF)], in_=res[:])
 
-        add_store(0, 0)
-        add_store(1, 0)
-        scatter(2)
-        add_store(0, 1)
-        add_store(1, 1)
-        add_store(2, 0)
-        add_store(2, 1)
-        scatter(3)
-        add_store(3, 0)
-        add_store(3, 1)
+        for k in range(POOL_TILES):
+            scatter(k)
+        for k in range(POOL_TILES):
+            sum_on_pool(k)
+        for k in range(POOL_TILES, TILES):
+            scatter(k)
+        for h in range(2):
+            for k in range(POOL_TILES, TILES):
+                sum_on_vector(k, h)

@@ -195,11 +195,12 @@ def tile_attend_bvbetween_s_kernel(
             nc.vector.tensor_scalar(
                 w_rows[:, r, :], probs[:, r, :], inv[:, r : r + 1], qs_cols[:, r : r + 1], ALU.mult, ALU.mult
             )
-        w_bf = sb([P, I, PACK], BF16, "w_bf")
+        staged = sb([P, 2, I * PACK], BF16, "staged")
+        w_bf = staged[:, 0, :].rearrange("p (i r) -> p i r", r=PACK)
         nc.vector.tensor_copy(
-            w_bf[:].rearrange("p (c i) r -> p c r i", i=PACK), w_rows[:].rearrange("p r (c i) -> p c r i", i=PACK)
+            w_bf.rearrange("p (c i) r -> p c r i", i=PACK), w_rows[:].rearrange("p r (c i) -> p c r i", i=PACK)
         )
-        w_codes, w_scales = quantise("w", w_bf[:].rearrange("p i r -> p (i r)"))
+        w_codes, w_scales = quantise("w", staged[:, 0, :])
 
         small_bank = bank("small_bank", "misc")
         turn(small_bank[:, 0:P], small_rows[:])
@@ -226,11 +227,12 @@ def tile_attend_bvbetween_s_kernel(
         g_scales = sb([P, E], U8, "g_scales")
         g_src = g_raw[:].rearrange("p j (n c i) -> p n c j i", n=TILES, i=PACK)
         for u in range(2):
-            g_bf = sb([P, 2, P, PACK], BF16, "g_bf%d" % u)
+            g_flat = staged[:, 1, :] if u else sb([P, 2 * P * PACK], BF16, "g_first")[:]
+            g_bf = g_flat.rearrange("p (v e j) -> p v e j", v=2, j=PACK)
             for v in range(2):
                 nc.scalar.copy(g_bf[:, v].rearrange("p (c i) j -> p c j i", i=PACK), g_src[:, 2 * u + v])
             cols = span(u, 2 * P)
-            quantise("g", g_bf[:].rearrange("p v e j -> p (v e j)"), g_codes[:, cols], g_scales[:, cols])
+            quantise("g", g_flat, g_codes[:, cols], g_scales[:, cols])
 
         grads = [bank("grads%d" % u, "prod") for u in range(2)]
         for k in range(TILES):
@@ -274,12 +276,12 @@ def tile_attend_bvbetween_s_kernel(
             nc.vector.tensor_copy(put[k][:].indirect(list1[:]), gs[:])
 
         def sum_on_pool(k):
-            kept = sb([P, T], F32, "kept%d" % k, "w_bf" if k == 0 else None)
+            kept = sb([P, T], F32, "kept%d" % k, "staged" if k == 0 else None)
             nc.gpsimd.tensor_tensor(kept[:], old_pool[k][:], fade_rows[:], ALU.mult)
             for h in range(2):
                 res = sb([P, HALF], F32, "res%d_%d" % (k, h))
                 nc.gpsimd.tensor_tensor(res[:], kept[:, span(h, HALF)], put[k][:, span(h, HALF)], ALU.add)
-                nc.scalar.dma_start(out=out[span(k, P), span(h, HALF)], in_=res[:])
+                nc.sync.dma_start(out=out[span(k, P), span(h, HALF)], in_=res[:])
 
         def sum_on_vector(k, h):
             back = bank("back%d_%d" % (k, h), "mix")
@@ -287,7 +289,7 @@ def tile_attend_bvbetween_s_kernel(
                 turn(back[:, span(j, P)], faded[4 * h + j][:, span(k - POOL_TILES, P)])
             res = sb([P, HALF], F32, "res%d_%d" % (k, h))
             nc.vector.tensor_tensor(res[:], back[:], put[k][:, span(h, HALF)], ALU.add)
-            nc.sync.dma_start(out=out[span(k, P), span(h, HALF)], in_=res[:])
+            nc.scalar.dma_start(out=out[span(k, P), span(h, HALF)], in_=res[:])
 
         for k in range(POOL_TILES):
             scatter(k)

@@ -24,9 +24,10 @@ BANK = 512
 TILES = E // P
 HALF = T // 2
 BLOCKS = T // P
+PER_BANK = HALF // P
 POOL_TILES = 2
 TURNED = TILES - POOL_TILES
-QUERY_SPLIT = 64
+QUERY_SPLIT = 32
 
 
 def tile_attend_bvbetween_s_kernel(
@@ -50,20 +51,19 @@ def tile_attend_bvbetween_s_kernel(
             nc.tensor.matmul(dst, lhsT=src, rhs=ident[:], start=start, stop=stop, is_transpose=True)
 
         def turn_sum(dst, first, second):
-            for b in range(2):
-                turn(dst[:, span(b, P)], first[:, span(b, P)], True, False)
-                turn(dst[:, span(b, P)], second[:, span(b, P)], False, True)
+            for n in range(2):
+                turn(dst[:, span(n, P)], first[:, span(n, P)], True, False)
+                turn(dst[:, span(n, P)], second[:, span(n, P)], False, True)
 
         def spread(dst, cols):
             for c in range(cols.shape[1]):
                 turn(dst[:, span(c, P)], cols[:, c : c + 1].to_broadcast([P, P]))
 
-        def quantise(name, src, codes=None, scales=None):
-            if codes is None:
-                codes = sb([P, src.shape[1] // PACK], U32, name + "_codes")[:]
-                scales = sb([P, src.shape[1] // PACK], U8, name + "_scales")[:]
+        def mx_tiles(name, columns):
+            return sb([P, columns], U32, name + "_codes")[:], sb([P, columns], U8, name + "_scales")[:]
+
+        def quantise(codes, scales, src):
             nc.vector.quantize_mx(out=codes.bitcast(FP8X4), scales=scales, in_=src)
-            return codes, scales
 
         list1 = sb([P, I // 16], U16, "list1")
         list2 = sb([P, I // 16], U16, "list2")
@@ -79,33 +79,31 @@ def tile_attend_bvbetween_s_kernel(
         old_turn = [sb([P, TURNED, HALF], F32, "old_turn%d" % h) for h in range(2)]
         put = [sb([P, T], F32, "put%d" % k) for k in range(TILES)]
         ident = sb([P, P], F32, "ident")
-        warm = sb([P, 8], F32, "warm")
-        warm_out = sb([P, 8], F32, "warm_out")
+        zeros = sb([P, 1], F32, "zeros")
 
         nc.vector.memset(key_bytes[:].bitcast(I32), 0)
-        nc.vector.memset(warm[:], 0.0)
-        nc.vector.memset(small_rows[:], 0.0)
-        nc.scalar.activation(warm_out[:], warm[:], ACT.Exp)
+        nc.vector.memset(zeros[:], 0.0)
+        nc.scalar.activation(small_rows[:], zeros[:].to_broadcast([P, P]), ACT.Copy)
         make_identity(nc, ident[:])
 
         def load_val(k):
             nc.sync.dma_start(out=val[k][:], in_=vals[span(k, P), :])
 
-        nc.sync.dma_start(out=fr_pairs[:], in_=fr.rearrange("o (p h) -> p (o h)", h=2))
+        nc.sync.dma_start(out=fr_pairs[:], in_=fr.rearrange("o (p m) -> p (o m)", m=2))
         nc.sync.dma_start(list1[:], offs)
         nc.sync.dma_start(list2[:], offs2)
         load_val(0)
         nc.sync.dma_start(out=key_words[:].bitcast(I32), in_=keys_words[0].bitcast(I32))
         load_val(1)
-        for g in range(4):
+        for quad in range(4):
             nc.sync.dma_start(
-                out=key_bytes[32 * g : 32 * g + 4, :].bitcast(I32), in_=keys_scales[0, span(g, 4), :].bitcast(I32)
+                out=key_bytes[32 * quad : 32 * quad + 4, :].bitcast(I32), in_=keys_scales[0, span(quad, 4), :].bitcast(I32)
             )
         nc.sync.dma_start(out=q_raw[:], in_=query.rearrange("(p j) q -> p j q", j=PACK))
         load_val(2)
         nc.sync.dma_start(out=g_raw[:], in_=grows.rearrange("(p j) e -> p j e", j=PACK))
-        nc.sync.dma_start(out=small_rows[BLOCKS : BLOCKS + 2, :], in_=sg.rearrange("o (j p) -> (o j) p", p=P))
-        nc.sync.dma_start(out=small_rows[0:BLOCKS, :], in_=fade.rearrange("o (j p) -> (o j) p", p=P))
+        nc.sync.dma_start(out=small_rows[BLOCKS : BLOCKS + 2, :], in_=sg.rearrange("o (n p) -> (o n) p", p=P))
+        nc.sync.dma_start(out=small_rows[0:BLOCKS, :], in_=fade.rearrange("o (n p) -> (o n) p", p=P))
         nc.sync.dma_start(out=qs_cols[:], in_=qs.rearrange("(p r) o -> p (r o)", r=PACK))
         load_val(3)
         for k in range(POOL_TILES):
@@ -123,9 +121,9 @@ def tile_attend_bvbetween_s_kernel(
         share2 = sb([P, I], F32, "share2")
         fr_bank = bank("fr_bank", "misc")
         spread(fr_bank, fr_pairs[:])
-        fr_rows = fr_bank[:, 0:I].rearrange("p (h n) -> p n h", h=2)
-        nc.scalar.activation(share1[:].rearrange("p (n h) -> p n h", h=2), fr_rows, ACT.Copy, scale=0.5, bias=-0.5)
-        nc.scalar.activation(share2[:].rearrange("p (n h) -> p n h", h=2), fr_rows, ACT.Copy, scale=-0.5)
+        fr_rows = fr_bank[:, 0:I].rearrange("p (m n) -> p n m", m=2)
+        nc.scalar.activation(share1[:].rearrange("p (n m) -> p n m", m=2), fr_rows, ACT.Copy, scale=0.5, bias=-0.5)
+        nc.scalar.activation(share2[:].rearrange("p (n m) -> p n m", m=2), fr_rows, ACT.Copy, scale=-0.5)
 
         mix_bank = [None] * TILES
         curve = [None] * TILES
@@ -164,9 +162,10 @@ def tile_attend_bvbetween_s_kernel(
         q_dst = q_bf[:].rearrange("p r s j -> p s j r")
         nc.vector.tensor_copy(q_dst[:, 0:QUERY_SPLIT], q_src[:, 0:QUERY_SPLIT])
         nc.scalar.copy(q_dst[:, QUERY_SPLIT:P], q_src[:, QUERY_SPLIT:P])
-        q_codes, q_scales = quantise("q", q_bf[:].rearrange("p r s j -> p (r s j)"))
+        q_codes, q_scales = mx_tiles("q", Q)
+        quantise(q_codes, q_scales, q_bf[:].rearrange("p r s j -> p (r s j)"))
 
-        scores = [bank("scores%d" % b, "prod")[:].rearrange("p (u i) -> p u i", u=2) for b in range(2)]
+        scores = [bank("scores%d" % u, "prod")[:].rearrange("p (v i) -> p v i", v=2) for u in range(2)]
         for r in range(PACK):
             nc.tensor.matmul_mx(
                 out=scores[r // 2][:, r % 2, :],
@@ -179,13 +178,13 @@ def tile_attend_bvbetween_s_kernel(
             )
         sums = sb([P, PACK], F32, "sums")
         probs = sb([P, PACK, I], F32, "probs")
-        for b in range(2):
-            neg_max = sb([P, 2], F32, "neg_max%d" % b)
-            nc.vector.tensor_reduce(neg_max[:], scores[b], AX.X, ALU.max, negate=True)
-            for u in range(2):
-                r = 2 * b + u
+        for u in range(2):
+            neg_max = sb([P, 2], F32, "neg_max%d" % u)
+            nc.vector.tensor_reduce(neg_max[:], scores[u], AX.X, ALU.max, negate=True)
+            for v in range(2):
+                r = 2 * u + v
                 nc.scalar.activation(
-                    probs[:, r, :], scores[b][:, u, :], ACT.Exp, bias=neg_max[:, u : u + 1], accum_out=sums[:, r : r + 1]
+                    probs[:, r, :], scores[u][:, v, :], ACT.Exp, bias=neg_max[:, v : v + 1], accum_out=sums[:, r : r + 1]
                 )
 
         inv = sb([P, PACK], F32, "inv")
@@ -200,7 +199,8 @@ def tile_attend_bvbetween_s_kernel(
         nc.vector.tensor_copy(
             w_bf.rearrange("p (c i) r -> p c r i", i=PACK), w_rows[:].rearrange("p r (c i) -> p c r i", i=PACK)
         )
-        w_codes, w_scales = quantise("w", staged[:, 0, :])
+        w_codes, w_scales = mx_tiles("w", I)
+        quantise(w_codes, w_scales, staged[:, 0, :])
 
         small_bank = bank("small_bank", "misc")
         turn(small_bank[:, 0:P], small_rows[:])
@@ -213,6 +213,12 @@ def tile_attend_bvbetween_s_kernel(
         half_gain = sb([P, I], F32, "half_gain")
         nc.scalar.activation(half_gain[:], gain_bank[:, 0:I], ACT.Copy, scale=0.5)
 
+        fade_rows = sb([P, T], F32, "fade_rows")
+        for h in range(2):
+            rows = bank("fade_bank%d" % h, "misc")
+            spread(rows, fade_cols[:, span(h, PER_BANK)])
+            nc.scalar.copy(fade_rows[:, span(h, HALF)], rows[:])
+
         early = sb([P, 2, 3, I], F32, "early", "q_raw")
         for k in (0, 1):
             tanh_and_square(k, early[:, k])
@@ -223,16 +229,15 @@ def tile_attend_bvbetween_s_kernel(
         for k in (0, 1):
             finish_slope(k)
 
-        g_codes = sb([P, E], U32, "g_codes")
-        g_scales = sb([P, E], U8, "g_scales")
+        g_codes, g_scales = mx_tiles("g", E)
         g_src = g_raw[:].rearrange("p j (n c i) -> p n c j i", n=TILES, i=PACK)
         for u in range(2):
             g_flat = staged[:, 1, :] if u else sb([P, 2 * P * PACK], BF16, "g_first")[:]
             g_bf = g_flat.rearrange("p (v e j) -> p v e j", v=2, j=PACK)
             for v in range(2):
-                nc.scalar.copy(g_bf[:, v].rearrange("p (c i) j -> p c j i", i=PACK), g_src[:, 2 * u + v])
-            cols = span(u, 2 * P)
-            quantise("g", g_flat, g_codes[:, cols], g_scales[:, cols])
+                copy_op = nc.vector.tensor_copy if u + v == 0 else nc.scalar.copy
+                copy_op(g_bf[:, v].rearrange("p (c i) j -> p c j i", i=PACK), g_src[:, 2 * u + v])
+            quantise(g_codes[:, span(u, 2 * P)], g_scales[:, span(u, 2 * P)], g_flat)
 
         grads = [bank("grads%d" % u, "prod") for u in range(2)]
         for k in range(TILES):
@@ -251,24 +256,18 @@ def tile_attend_bvbetween_s_kernel(
             tanh_and_square(k, late[:, k - 2])
         for k in (2, 3):
             bend(k)
-
-        fade_rows = sb([P, T], F32, "fade_rows")
-        for h in range(2):
-            rows = bank("fade_bank%d" % h, "misc")
-            spread(rows, fade_cols[:, span(h, 4)])
-            nc.scalar.copy(fade_rows[:, span(h, HALF)], rows[:])
         for k in (2, 3):
             finish_slope(k)
 
         width = TURNED * P
-        faded = [sb([P, width], F32, "faded%d" % j) for j in range(BLOCKS)]
+        faded = [sb([P, width], F32, "faded%d" % n) for n in range(BLOCKS)]
         for pair in range(BLOCKS // 2):
             turned = bank("turned%d" % pair, "misc")
-            for j in (2 * pair, 2 * pair + 1):
-                for v in range(TURNED):
-                    turn(turned[:, span(j % 2 * TURNED + v, P)], old_turn[j // 4][:, v, span(j % 4, P)])
-            for j in (2 * pair, 2 * pair + 1):
-                nc.scalar.activation(faded[j][:], turned[:, span(j % 2, width)], ACT.Copy, scale=fade_cols[:, j : j + 1])
+            for n in (2 * pair, 2 * pair + 1):
+                for k in range(TURNED):
+                    turn(turned[:, span(n % 2 * TURNED + k, P)], old_turn[n // PER_BANK][:, k, span(n % PER_BANK, P)])
+            for n in (2 * pair, 2 * pair + 1):
+                nc.scalar.activation(faded[n][:], turned[:, span(n % 2, width)], ACT.Copy, scale=fade_cols[:, n : n + 1])
 
         def scatter(k):
             gs = sb([P, I], F32, "gs%d" % k)
@@ -285,8 +284,8 @@ def tile_attend_bvbetween_s_kernel(
 
         def sum_on_vector(k, h):
             back = bank("back%d_%d" % (k, h), "mix")
-            for j in range(4):
-                turn(back[:, span(j, P)], faded[4 * h + j][:, span(k - POOL_TILES, P)])
+            for n in range(PER_BANK):
+                turn(back[:, span(n, P)], faded[PER_BANK * h + n][:, span(k - POOL_TILES, P)])
             res = sb([P, HALF], F32, "res%d_%d" % (k, h))
             nc.vector.tensor_tensor(res[:], back[:], put[k][:, span(h, HALF)], ALU.add)
             nc.scalar.dma_start(out=out[span(k, P), span(h, HALF)], in_=res[:])

from contextlib import ExitStack

import concourse.mybir as mybir
from concourse.masks import make_identity

D, E, T, I, Q = 512, 512, 1024, 256, 512
FLOPS = 2 * Q * I * D + 2 * E * I * Q

F32 = mybir.dt.float32
BF16 = mybir.dt.bfloat16
I32 = mybir.dt.int32
U32 = mybir.dt.uint32
U16 = mybir.dt.uint16
U8 = mybir.dt.uint8
FP8X4 = mybir.dt.float8_e4m3fn_x4
FP4X4 = mybir.dt.float4_e2m1fn_x4
ALU = mybir.AluOpType
ACT = mybir.ActivationFunctionType
AX = mybir.AxisListType

P = 128
PACK = 4
BANK = 512
TILES = E // P
HALF = T // 2
BLOCKS = T // P
PER_BANK = HALF // P
POOL_TILES = 2
TURNED = TILES - POOL_TILES
QUERY_SPLIT = 32


def tile_attend_bvbetween_s_kernel(
    tc, query, qs, grows, vals, keys_words, keys_scales, fr, sg, old, fade, offs, offs2, out
):
    nc = tc.nc
    with ExitStack() as ctx:
        keep = ctx.enter_context(tc.tile_pool(name="keep", bufs=1))
        psum = ctx.enter_context(tc.psum_pool(name="psum", bufs=1))

        def sb(shape, dtype, name, on=None):
            return keep.tile(shape, dtype, name=name, tag=on or name, align_bytes=64)

        def bank(name, ring):
            return psum.tile([P, BANK], F32, name=name, tag=ring, bufs=4 if ring == "mix" else 2)

        def span(n, width):
            return slice(n * width, (n + 1) * width)

        def turn(dst, src, start=True, stop=True):
            nc.tensor.matmul(dst, lhsT=src, rhs=ident[:], start=start, stop=stop, is_transpose=True)

        def turn_sum(dst, first, second):
            for n in range(2):
                turn(dst[:, span(n, P)], first[:, span(n, P)], True, False)
                turn(dst[:, span(n, P)], second[:, span(n, P)], False, True)

        def spread(dst, cols):
            for c in range(cols.shape[1]):
                turn(dst[:, span(c, P)], cols[:, c : c + 1].to_broadcast([P, P]))

        def mx_tiles(name, columns):
            return sb([P, columns], U32, name + "_codes")[:], sb([P, columns], U8, name + "_scales")[:]

        def quantise(codes, scales, src):
            nc.vector.quantize_mx(out=codes.bitcast(FP8X4), scales=scales, in_=src)

        list1 = sb([P, I // 16], U16, "list1")
        list2 = sb([P, I // 16], U16, "list2")
        key_words = sb([P, T], U16, "key_words")
        key_bytes = sb([P, T], U8, "key_bytes")
        small_rows = sb([P, P], F32, "small_rows")
        fr_pairs = sb([P, 2], F32, "fr_pairs")
        q_raw = sb([P, PACK, Q], F32, "q_raw")
        g_raw = sb([P, PACK, E], F32, "g_raw")
        qs_cols = sb([P, PACK], F32, "qs_cols")
        val = [sb([P, T], F32, "val%d" % k) for k in range(TILES)]
        old_pool = [sb([P, T], F32, "old_pool%d" % k) for k in range(POOL_TILES)]
        old_turn = [sb([P, TURNED, HALF], F32, "old_turn%d" % h) for h in range(2)]
        put = [sb([P, T], F32, "put%d" % k) for k in range(TILES)]
        ident = sb([P, P], F32, "ident")
        zeros = sb([P, 1], F32, "zeros")

        nc.vector.memset(key_bytes[:].bitcast(I32), 0)
        nc.vector.memset(zeros[:], 0.0)
        nc.scalar.activation(small_rows[:], zeros[:].to_broadcast([P, P]), ACT.Copy)
        make_identity(nc, ident[:])

        def load_val(k):
            nc.sync.dma_start(out=val[k][:], in_=vals[span(k, P), :])

        nc.sync.dma_start(out=fr_pairs[:], in_=fr.rearrange("o (p m) -> p (o m)", m=2))
        nc.sync.dma_start(list1[:], offs)
        nc.sync.dma_start(list2[:], offs2)
        load_val(0)
        nc.sync.dma_start(out=key_words[:].bitcast(I32), in_=keys_words[0].bitcast(I32))
        load_val(1)
        for quad in range(4):
            nc.sync.dma_start(
                out=key_bytes[32 * quad : 32 * quad + 4, :].bitcast(I32), in_=keys_scales[0, span(quad, 4), :].bitcast(I32)
            )
        nc.sync.dma_start(out=q_raw[:], in_=query.rearrange("(p j) q -> p j q", j=PACK))
        load_val(2)
        nc.sync.dma_start(out=g_raw[:], in_=grows.rearrange("(p j) e -> p j e", j=PACK))
        nc.sync.dma_start(out=small_rows[BLOCKS : BLOCKS + 2, :], in_=sg.rearrange("o (n p) -> (o n) p", p=P))
        nc.sync.dma_start(out=small_rows[0:BLOCKS, :], in_=fade.rearrange("o (n p) -> (o n) p", p=P))
        nc.sync.dma_start(out=qs_cols[:], in_=qs.rearrange("(p r) o -> p (r o)", r=PACK))
        load_val(3)
        for k in range(POOL_TILES):
            nc.sync.dma_start(out=old_pool[k][:], in_=old[span(k, P), :])
        for h in range(2):
            nc.sync.dma_start(
                out=old_turn[h][:], in_=old[POOL_TILES * P : E, span(h, HALF)].rearrange("(k p) t -> p k t", p=P)
            )

        for k in range(2):
            nc.vector.memset(put[k][:].bitcast(I32), 0)
            nc.gpsimd.memset(put[2 + k][:], 0.0)

        share1 = sb([P, I], F32, "share1")
        share2 = sb([P, I], F32, "share2")
        fr_bank = bank("fr_bank", "misc")
        spread(fr_bank, fr_pairs[:])
        fr_rows = fr_bank[:, 0:I].rearrange("p (m n) -> p n m", m=2)
        nc.scalar.activation(share1[:].rearrange("p (n m) -> p n m", m=2), fr_rows, ACT.Copy, scale=0.5, bias=-0.5)
        nc.scalar.activation(share2[:].rearrange("p (n m) -> p n m", m=2), fr_rows, ACT.Copy, scale=-0.5)

        mix_bank = [None] * TILES
        curve = [None] * TILES
        slope = [None] * TILES

        def gather_vals(k):
            parts = sb([P, 2, I], F32, "parts%d" % k)
            nc.vector.tensor_tensor(parts[:, 0, :], val[k][:].indirect(list1[:]), share1[:], ALU.mult)
            nc.vector.tensor_tensor(parts[:, 1, :], val[k][:].indirect(list2[:]), share2[:], ALU.mult)
            mix_bank[k] = bank("mix%d" % k, "mix")
            turn_sum(mix_bank[k][:, 0:I], parts[:, 0, :], parts[:, 1, :])

        def tanh_and_square(k, room):
            curve[k] = room
            nc.scalar.activation(room[:, 0, :], mix_bank[k][:, 0:I], ACT.Tanh, scale=-1.0)
            nc.scalar.activation(room[:, 1, :], room[:, 0, :], ACT.Square)

        def bend(k):
            room = curve[k]
            nc.vector.scalar_tensor_tensor(room[:, 2, :], room[:, 1, :], 1.0, mix_bank[k][:, 0:I], ALU.subtract, ALU.mult)
            turn_sum(mix_bank[k][:, I:BANK], room[:, 0, :], room[:, 2, :])

        def finish_slope(k):
            slope[k] = sb([P, I], F32, "slope%d" % k)
            nc.vector.scalar_tensor_tensor(slope[k][:], mix_bank[k][:, I:BANK], 1.0, half_gain[:], ALU.add, ALU.mult)

        gather_vals(0)
        gather_vals(1)
        keys_w = sb([P, I], U16, "keys_w")
        keys_b = sb([P, I], U8, "keys_b")
        nc.vector.tensor_copy(keys_w[:], key_words[:].indirect(list1[:]))
        nc.vector.tensor_copy(keys_b[:], key_bytes[:].indirect(list1[:]))

        q_bf = sb([P, PACK, P, PACK], BF16, "q_bf")
        q_src = q_raw[:].rearrange("p j (s r) -> p s j r", r=PACK)
        q_dst = q_bf[:].rearrange("p r s j -> p s j r")
        nc.vector.tensor_copy(q_dst[:, 0:QUERY_SPLIT], q_src[:, 0:QUERY_SPLIT])
        nc.scalar.copy(q_dst[:, QUERY_SPLIT:P], q_src[:, QUERY_SPLIT:P])
        q_codes, q_scales = mx_tiles("q", Q)
        quantise(q_codes, q_scales, q_bf[:].rearrange("p r s j -> p (r s j)"))

        scores = [bank("scores%d" % u, "prod")[:].rearrange("p (v i) -> p v i", v=2) for u in range(2)]
        for r in range(PACK):
            nc.tensor.matmul_mx(
                out=scores[r // 2][:, r % 2, :],
                lhsT=q_codes[:, span(r, P)].bitcast(FP8X4),
                lhsT_scale=q_scales[:, span(r, P)],
                rhs=keys_w[:].bitcast(FP4X4),
                rhs_scale=keys_b[:],
                start=True,
                stop=True,
            )
        sums = sb([P, PACK], F32, "sums")
        probs = sb([P, PACK, I], F32, "probs")
        for u in range(2):
            neg_max = sb([P, 2], F32, "neg_max%d" % u)
            nc.vector.tensor_reduce(neg_max[:], scores[u], AX.X, ALU.max, negate=True)
            for v in range(2):
                r = 2 * u + v
                nc.scalar.activation(
                    probs[:, r, :], scores[u][:, v, :], ACT.Exp, bias=neg_max[:, v : v + 1], accum_out=sums[:, r : r + 1]
                )

        inv = sb([P, PACK], F32, "inv")
        nc.vector.reciprocal(inv[:], sums[:])
        w_rows = sb([P, PACK, I], BF16, "w_rows")
        for r in range(PACK):
            nc.vector.tensor_scalar(
                w_rows[:, r, :], probs[:, r, :], inv[:, r : r + 1], qs_cols[:, r : r + 1], ALU.mult, ALU.mult
            )
        staged = sb([P, 2, I * PACK], BF16, "staged")
        w_bf = staged[:, 0, :].rearrange("p (i r) -> p i r", r=PACK)
        nc.vector.tensor_copy(
            w_bf.rearrange("p (c i) r -> p c r i", i=PACK), w_rows[:].rearrange("p r (c i) -> p c r i", i=PACK)
        )
        w_codes, w_scales = mx_tiles("w", I)
        quantise(w_codes, w_scales, staged[:, 0, :])

        small_bank = bank("small_bank", "misc")
        turn(small_bank[:, 0:P], small_rows[:])
        gain_cols = sb([P, 2], F32, "gain_cols")
        fade_cols = sb([P, BLOCKS], F32, "fade_cols")
        nc.scalar.copy(gain_cols[:], small_bank[:, BLOCKS : BLOCKS + 2])
        nc.scalar.copy(fade_cols[:], small_bank[:, 0:BLOCKS])
        gain_bank = bank("gain_bank", "misc")
        spread(gain_bank, gain_cols[:])
        half_gain = sb([P, I], F32, "half_gain")
        nc.scalar.activation(half_gain[:], gain_bank[:, 0:I], ACT.Copy, scale=0.5)

        fade_rows = sb([P, T], F32, "fade_rows")
        for h in range(2):
            rows = bank("fade_bank%d" % h, "misc")
            spread(rows, fade_cols[:, span(h, PER_BANK)])
            nc.scalar.copy(fade_rows[:, span(h, HALF)], rows[:])

        early = sb([P, 2, 3, I], F32, "early", "q_raw")
        for k in (0, 1):
            tanh_and_square(k, early[:, k])
        gather_vals(2)
        gather_vals(3)
        for k in (0, 1):
            bend(k)
        for k in (0, 1):
            finish_slope(k)

        g_codes, g_scales = mx_tiles("g", E)
        g_src = g_raw[:].rearrange("p j (n c i) -> p n c j i", n=TILES, i=PACK)
        for u in range(2):
            g_flat = staged[:, 1, :] if u else sb([P, 2 * P * PACK], BF16, "g_first")[:]
            g_bf = g_flat.rearrange("p (v e j) -> p v e j", v=2, j=PACK)
            for v in range(2):
                copy_op = nc.vector.tensor_copy if u + v == 0 else nc.scalar.copy
                copy_op(g_bf[:, v].rearrange("p (c i) j -> p c j i", i=PACK), g_src[:, 2 * u + v])
            quantise(g_codes[:, span(u, 2 * P)], g_scales[:, span(u, 2 * P)], g_flat)

        grads = [bank("grads%d" % u, "prod") for u in range(2)]
        for k in range(TILES):
            nc.tensor.matmul_mx(
                out=grads[k // 2][:, span(k % 2, I)],
                lhsT=g_codes[:, span(k, P)].bitcast(FP8X4),
                lhsT_scale=g_scales[:, span(k, P)],
                rhs=w_codes.bitcast(FP8X4),
                rhs_scale=w_scales,
                start=True,
                stop=True,
            )

        late = sb([P, 2, 3, I], F32, "late")
        for k in (2, 3):
            tanh_and_square(k, late[:, k - 2])
        for k in (2, 3):
            bend(k)
        for k in (2, 3):
            finish_slope(k)

        width = TURNED * P
        faded = [sb([P, width], F32, "faded%d" % n) for n in range(BLOCKS)]
        for pair in range(BLOCKS // 2):
            turned = bank("turned%d" % pair, "misc")
            for n in (2 * pair, 2 * pair + 1):
                for k in range(TURNED):
                    turn(turned[:, span(n % 2 * TURNED + k, P)], old_turn[n // PER_BANK][:, k, span(n % PER_BANK, P)])
            for n in (2 * pair, 2 * pair + 1):
                nc.scalar.activation(faded[n][:], turned[:, span(n % 2, width)], ACT.Copy, scale=fade_cols[:, n : n + 1])

        def scatter(k):
            gs = sb([P, I], F32, "gs%d" % k)
            nc.vector.tensor_tensor(gs[:], grads[k // 2][:, span(k % 2, I)], slope[k][:], ALU.mult)
            nc.vector.tensor_copy(put[k][:].indirect(list1[:]), gs[:])

        def sum_on_pool(k):
            kept = sb([P, T], F32, "kept%d" % k, "staged" if k == 0 else None)
            nc.gpsimd.tensor_tensor(kept[:], old_pool[k][:], fade_rows[:], ALU.mult)
            for h in range(2):
                res = sb([P, HALF], F32, "res%d_%d" % (k, h))
                nc.gpsimd.tensor_tensor(res[:], kept[:, span(h, HALF)], put[k][:, span(h, HALF)], ALU.add)
                nc.sync.dma_start(out=out[span(k, P), span(h, HALF)], in_=res[:])

        def sum_on_vector(k, h):
            back = bank("back%d_%d" % (k, h), "mix")
            for n in range(PER_BANK):
                turn(back[:, span(n, P)], faded[PER_BANK * h + n][:, span(k - POOL_TILES, P)])
            res = sb([P, HALF], F32, "res%d_%d" % (k, h))
            nc.vector.tensor_tensor(res[:], back[:], put[k][:, span(h, HALF)], ALU.add)
            nc.scalar.dma_start(out=out[span(k, P), span(h, HALF)], in_=res[:])

        for k in range(POOL_TILES):
            scatter(k)
        for k in range(POOL_TILES):
            sum_on_pool(k)
        for k in range(POOL_TILES, TILES):
            scatter(k)
        for h in range(2):
            for k in range(POOL_TILES, TILES):
                sum_on_vector(k, h)
